import numpy as np
import ml_dtypes


def mxq(x, axis, fmt="e4m3"):
    dtype, down = {"e4m3": (ml_dtypes.float8_e4m3fn, 7), "e5m2": (ml_dtypes.float8_e5m2, 14)}[fmt]
    v = np.moveaxis(np.asarray(x, np.float32).astype(ml_dtypes.bfloat16).astype(np.float64), axis, -1)
    blocks = v.reshape(v.shape[:-1] + (-1, 32))
    amax = np.abs(blocks).max(-1, keepdims=True)
    byte = np.maximum(np.where(amax > 0, np.frexp(amax)[1] - 1 + 127, 0) - down, 1)
    scale = np.exp2(byte - 127.0)
    codes = (blocks / scale).astype(np.float32).astype(dtype).astype(np.float64)
    return np.moveaxis((codes * scale).reshape(v.shape), -1, axis)


WIDE = False


def mx_kscale(k):
    if not WIDE:
        return np.ones(k)
    levels = np.array([10, -10, 5, -5, 0])
    if k % 512:
        return np.exp2(np.random.permutation(np.resize(levels, k // 32))).repeat(32)
    a = np.empty((k // 512, 16))
    for p in range(k // 512):
        a[p, :8] = np.random.permutation(np.resize(levels, 8))
        for g in range(8):
            far = levels[np.abs(levels - a[p, g]) >= 10]
            a[p, g + 8] = far[np.random.randint(len(far))]
    return np.exp2(a.ravel()).repeat(32)


def f64(x):
    return np.asarray(x).astype(np.float64)


def striped(idx):
    return np.tile(np.asarray(idx).reshape(-1, 16).T, (8, 1)).astype(np.uint16)


def unstriped(offs):
    return offs[:16].T.reshape(-1).astype(np.int64)


E2M1 = np.array([0.0, 0.5, 1.0, 1.5, 2.0, 3.0, 4.0, 6.0, -0.0, -0.5, -1.0, -1.5, -2.0, -3.0, -4.0, -6.0])


def pack_weight(w, fmt):
    k, n = w.shape
    w = f64(np.asarray(w, np.float32).astype(ml_dtypes.bfloat16)).reshape(k // 32, 32, n)
    amax = np.abs(w).max(1)
    if fmt == "e4m3":
        byte = np.frexp(amax)[1] - 1 + 127 - 7
    else:
        mant, ex = np.frexp(amax / 6.0)
        byte = np.where(mant > 0.5, ex, ex - 1) + 127
    byte = np.clip(np.where(amax > 0, byte, 1), 1, 254)
    scaled = (w * np.exp2(127.0 - byte)[:, None, :]).reshape(k, n).astype(np.float32)
    by_word = np.ascontiguousarray(scaled.reshape(k // 512, 128, 4, n).transpose(0, 1, 3, 2))
    if fmt == "e4m3":
        words = by_word.astype(ml_dtypes.float8_e4m3fn).view(np.uint8)
    else:
        c = by_word.astype(ml_dtypes.float4_e2m1fn).view(np.uint8) & 0xF
        words = (c[..., 0::2] | (c[..., 1::2] << 4)).reshape(k // 512, 128, 2 * n)
    return np.ascontiguousarray(words), np.ascontiguousarray(byte.astype(np.uint8).reshape(k // 512, 16, n))


def unpack_weight(words, scales, fmt):
    g, _, n = scales.shape
    words = np.ascontiguousarray(words).reshape(g, 128, n, -1)
    if fmt == "e4m3":
        vals = words.view(ml_dtypes.float8_e4m3fn).astype(np.float64)
    else:
        nib = np.empty((g, 128, n, 4), np.uint8)
        nib[..., 0::2] = words & 0xF
        nib[..., 1::2] = words >> 4
        vals = E2M1[nib]
    vals = vals * np.repeat(np.exp2(scales.astype(np.float64) - 127.0), 8, axis=1)[..., None]
    return vals.transpose(0, 1, 3, 2).reshape(g * 512, n)


def sigmoid(v):
    return 1.0 / (1.0 + np.exp(-v))


def sgn(shape):
    return np.random.uniform(0.5, 2.0, shape) * np.where(np.random.standard_normal(shape) < 0, -1.0, 1.0)


K, T, J, R, F, Z, O, U, D, N, L, E = 512, 1024, 256, 512, 512, 1024, 128, 128, 256, 256, 512, 1024


def setup_inputs():
    n = np.random.standard_normal
    idx = np.random.permutation(T)[:J]
    idx2 = np.random.permutation(Z)[:J]
    idx3 = np.random.permutation(J)[:O]
    idx4 = np.random.permutation(J)[:O]
    idx5 = np.random.permutation(J)[:U]
    idx6 = np.random.permutation(J)[:U]
    idx7 = np.random.permutation(E)[:D]
    ff = mx_kscale(F)
    fk = mx_kscale(K)
    fr = mx_kscale(R)
    fl = mx_kscale(L)
    xop = pack_weight(n((F, Z)) / ff[:, None], "e4m3")
    wp = pack_weight(n((K, R)) * 1 / np.sqrt(K) / fk[:, None], "e2m1")
    w2p = pack_weight(n((F, R)) * 1 / np.sqrt(F) * ff[:, None], "e2m1")
    wbp = pack_weight(n((R, N)) * 1 / np.sqrt(R) / fr[:, None], "e2m1")
    sxp = pack_weight(n((L, D)) / fl[:, None], "e4m3")
    wsp = pack_weight(n((L, N)) * 1 / np.sqrt(L) * fl[:, None], "e2m1")
    return {
        "xo_words": xop[0],
        "xo_scales": xop[1],
        "cq": (np.random.randint(-7, 8, (K, T)).astype(np.float64)).astype(np.float32),
        "gs": (np.random.uniform(0.1, 0.4, (K, 1)) * fk[:, None]).astype(np.float32),
        "w_words": wp[0],
        "w_scales": wp[1],
        "w2_words": w2p[0],
        "w2_scales": w2p[1],
        "sa": (np.random.uniform(0.5, 1.6, (R, 1)) * fr[:, None]).astype(np.float32),
        "sb": (np.random.uniform(0.5, 1.6, (R, 1)) * fr[:, None]).astype(np.float32),
        "sg": (sgn((R, 1))).astype(np.float32),
        "bg": (np.random.uniform(-2.0, 2.0, (R, 1))).astype(np.float32),
        "sh": (sgn((R, 1))).astype(np.float32),
        "bh": (np.random.uniform(-2.0, 2.0, (R, 1))).astype(np.float32),
        "wb_words": wbp[0],
        "wb_scales": wbp[1],
        "sx_words": sxp[0],
        "sx_scales": sxp[1],
        "ws_words": wsp[0],
        "ws_scales": wsp[1],
        "offs": striped(idx),
        "offs2": striped(idx2),
        "offs3": striped(idx3),
        "offs4": striped(idx4),
        "offs5": striped(idx5),
        "offs6": striped(idx6),
        "offs7": striped(idx7),
    }


def reference(xo_words, xo_scales, cq, gs, w_words, w_scales, w2_words, w2_scales, sa, sb, sg, bg, sh, bh, wb_words, wb_scales, sx_words, sx_scales, ws_words, ws_scales, offs, offs2, offs3, offs4, offs5, offs6, offs7):
    idx = unstriped(offs)
    idx2 = unstriped(offs2)
    idx3 = unstriped(offs3)
    idx4 = unstriped(offs4)
    idx5 = unstriped(offs5)
    idx6 = unstriped(offs6)
    idx7 = unstriped(offs7)
    xou = unpack_weight(xo_words, xo_scales, "e4m3")
    wu = unpack_weight(w_words, w_scales, "e2m1")
    w2u = unpack_weight(w2_words, w2_scales, "e2m1")
    wbu = unpack_weight(wb_words, wb_scales, "e2m1")
    sxu = unpack_weight(sx_words, sx_scales, "e4m3")
    wsu = unpack_weight(ws_words, ws_scales, "e2m1")
    x1 = f64(cq)[:, idx] * f64(gs)
    x1q = mxq(x1, 0, "e4m3")
    a = wu.T @ x1q
    xoidx2g = xou[:, idx2]
    b = w2u.T @ xoidx2g
    h1 = a[:, idx3] * f64(sa) * sigmoid(a[:, idx4] * f64(sg) + f64(bg))
    h2 = b[:, idx5] * f64(sb) * sigmoid(b[:, idx6] * f64(sh) + f64(bh))
    hid = np.concatenate([h1, h2], axis=1)
    hidq = mxq(hid, 0, "e4m3")
    p = wbu.T @ hidq + wsu.T @ sxu
    y = np.zeros((N, E))
    y[:, idx7] = p
    return y

@@ -1,0 +1,300 @@
+from contextlib import ExitStack
+
+import concourse.mybir as mybir
+
+K, T, J, R, Z, HALF, D, N, E = 512, 1024, 256, 512, 1024, 128, 256, 256, 1024
+FLOPS = 2 * (K * R * J + K * R * J + R * N * D + K * N * D)
+
+F32 = mybir.dt.float32
+BF16 = mybir.dt.bfloat16
+I32 = mybir.dt.int32
+U32 = mybir.dt.uint32
+U16 = mybir.dt.uint16
+U8 = mybir.dt.uint8
+FP8X4 = mybir.dt.float8_e4m3fn_x4
+FP4X4 = mybir.dt.float4_e2m1fn_x4
+COPY = mybir.ActivationFunctionType.Copy
+SIGMOID = mybir.ActivationFunctionType.Sigmoid
+MULT = mybir.AluOpType.mult
+
+P = 128
+PACK = 4
+QUADS = 4
+ALIGN = 64
+
+
+def tile_list_gatedsides_codednote_further_scattered_kernel(
+    tc, xo_words, xo_scales, cq, gs, w_words, w_scales, w2_words, w2_scales, sa, sb, sg, bg, sh, bh,
+    wb_words, wb_scales, sx_words, sx_scales, ws_words, ws_scales,
+    offs, offs2, offs3, offs4, offs5, offs6, offs7, out,
+):
+    nc = tc.nc
+    with ExitStack() as ctx:
+        held = ctx.enter_context(tc.tile_pool(name="held", bufs=1))
+        psum = ctx.enter_context(tc.psum_pool(name="psum", bufs=1))
+
+        def load_list(src, name):
+            tile = held.tile(list(src.shape), U16, name=name)
+            nc.sync.dma_start(tile[:], src)
+            return tile
+
+        def load_bytes(src, name):
+            tile = held.tile(list(src.shape), U8, name=name, tag=name, align_bytes=ALIGN)
+            nc.sync.dma_start(tile[:].bitcast(I32), src.bitcast(I32))
+            return tile
+
+        def load_per_row(queue, src, name):
+            tile = held.tile([P, PACK], F32, name=name)
+            queue.dma_start(tile[:], src.rearrange("(p t) o -> p (t o)", t=PACK))
+            return tile
+
+        def scale_rows(src):
+            return src[0].bitcast(I32).rearrange("(q r) c -> r q c", r=4)
+
+        def stage_scales(queue, src, name):
+            tile = held.tile([4, QUADS, src.shape[2] // 4], I32, name=name)
+            queue.dma_start(tile[:], scale_rows(src))
+            return tile
+
+        def zeroed_plane(width, name, tag=""):
+            tile = held.tile([P, width], U8, name=name, tag=tag or name, align_bytes=ALIGN)
+            nc.vector.memset(tile[:].bitcast(I32), 0)
+            return tile
+
+        def spread(plane, staged):
+            for q in range(QUADS):
+                nc.vector.tensor_copy(plane[32 * q : 32 * q + 4, :].bitcast(I32), staged[:, q, :])
+
+        def deal(copy, src, dtype, name):
+            tile = held.tile(list(src.shape), U8, name=name, tag=name, align_bytes=ALIGN)
+            src_v, dst_v = src[:], tile[:]
+            if dtype is not U8:
+                src_v, dst_v = src_v.bitcast(dtype), dst_v.bitcast(dtype)
+            copy(
+                dst_v.rearrange("p (t m) -> p t m", t=PACK), src_v.rearrange("p (m t) -> p t m", t=PACK)
+            )
+            return tile
+
+        warm_in = held.tile([P, 1], F32, name="warm_in")
+        warm_out = held.tile([P, 1], F32, name="warm_out")
+        nc.vector.memset(warm_in[:], 0.0)
+        nc.scalar.activation(out=warm_out[:], in_=warm_in[:], func=SIGMOID)
+
+        def zeroed_page(name):
+            page = held.tile([P, E], F32, name=name)
+            nc.vector.memset(page[:].bitcast(I32), 0)
+            return page
+
+        xo_plane = zeroed_plane(Z, "xo_plane")
+        w2_plane = zeroed_plane(R, "w2_plane")
+        w_plane = zeroed_plane(R, "w_plane")
+        pages = [zeroed_page(f"page{n}") for n in range(2)]
+
+        cq_rows = cq.rearrange("(p t) c -> t p c", t=PACK)
+
+        def load_cq(t):
+            tile = held.tile([P, T], F32, name=f"cq{t}", tag=f"cq{t}")
+            nc.sync.dma_start(tile[:], cq_rows[t])
+            return tile
+
+        idx2 = load_list(offs2, "idx2")
+        xo_staged = stage_scales(nc.sync, xo_scales, "xo_staged")
+        w2_staged = stage_scales(nc.sync, w2_scales, "w2_staged")
+        w2_w = load_bytes(w2_words[0], "w2_w")
+        xo_w = load_bytes(xo_words[0].rearrange("p z t -> p (z t)"), "xo_w")
+        idx = load_list(offs, "idx")
+        gs_t = load_per_row(nc.sync, gs, "gs_t")
+        cq_t = [load_cq(0), load_cq(1)]
+        w_staged = stage_scales(nc.sync, w_scales, "w_staged")
+        w_w = load_bytes(w_words[0], "w_w")
+        idx6 = load_list(offs6, "idx6")
+        idx5 = load_list(offs5, "idx5")
+        cq_t.extend([load_cq(2), load_cq(3)])
+        last_staged = held.tile([4, QUADS, 3, N // 4], I32, name="last_staged")
+        for i, src in enumerate((wb_scales, ws_scales, sx_scales)):
+            nc.sync.dma_start(last_staged[:, :, i, :], scale_rows(src))
+        ws_w = load_bytes(ws_words[0], "ws_w")
+        sx_w = load_bytes(sx_words[0].rearrange("p d t -> p (d t)"), "sx_w")
+        wb_w = load_bytes(wb_words[0], "wb_w")
+        idx4 = load_list(offs4, "idx4")
+        idx3 = load_list(offs3, "idx3")
+        idx7 = load_list(offs7, "idx7")
+
+        sh_t = load_per_row(nc.gpsimd, sh, "sh_t")
+        bh_t = load_per_row(nc.gpsimd, bh, "bh_t")
+        sb_t = load_per_row(nc.gpsimd, sb, "sb_t")
+        sg_t = load_per_row(nc.gpsimd, sg, "sg_t")
+        bg_t = load_per_row(nc.gpsimd, bg, "bg_t")
+        sa_t = load_per_row(nc.gpsimd, sa, "sa_t")
+
+        def first_product(acc, words, plane, codes, scales, t):
+            nc.tensor.matmul_mx(
+                out=acc,
+                lhsT=words[:, 2 * P * t : 2 * P * (t + 1)].bitcast(FP4X4),
+                lhsT_scale=plane[:, P * t : P * (t + 1)],
+                rhs=codes.bitcast(FP8X4),
+                rhs_scale=scales,
+                start=True,
+                stop=True,
+            )
+
+        def rows_of(copy, acc, name, tag=""):
+            tile = held.tile([P, J], F32, name=name, tag=tag or name)
+            copy(tile[:], acc[:])
+            return tile
+
+        def look_up_gated(looked, rows, t, value_idx, weight, gate_idx, slope, offset):
+            nc.scalar.activation(
+                out=looked[:, 0, t % 2, :], in_=rows[:].indirect(gate_idx[:]), func=SIGMOID,
+                bias=offset[:, t : t + 1], scale=slope[:, t : t + 1],
+            )
+            nc.scalar.activation(
+                out=looked[:, 1, t % 2, :], in_=rows[:].indirect(value_idx[:]), func=COPY, scale=weight[:, t : t + 1],
+            )
+
+        def gate(hid, looked, first):
+            nc.vector.tensor_tensor(
+                hid[:, :, first : first + 2].rearrange("p (c i) t -> p c t i", i=2),
+                looked[:, 1, :, :].rearrange("p t (c i) -> p c t i", i=2),
+                looked[:, 0, :, :].rearrange("p t (c i) -> p c t i", i=2),
+                MULT,
+            )
+
+        def quantise(src, codes, scales):
+            nc.vector.quantize_mx(out=codes.bitcast(FP8X4), scales=scales, in_=src[:].rearrange("p c t -> p (c t)"))
+
+        def quantise_hid(hid, name):
+            codes = held.tile([P, HALF], U32, name=f"{name}_codes", align_bytes=ALIGN)
+            scales = held.tile([P, HALF], U8, name=f"{name}_scales", align_bytes=ALIGN)
+            quantise(hid, codes[:], scales[:])
+            return codes, scales
+
+        spread(xo_plane, xo_staged)
+        xo_scales_g = held.tile([P, J], U8, name="xo_scales_g", align_bytes=ALIGN)
+        nc.vector.tensor_copy(xo_scales_g[:], xo_plane[:].indirect(idx2[:]))
+        spread(w2_plane, w2_staged)
+        w2_plane_d = deal(nc.vector.tensor_copy, w2_plane, U8, "w2_plane_d")
+        xo_codes_g = held.tile([P, J], U32, name="xo_codes_g", align_bytes=ALIGN)
+        nc.vector.tensor_copy(xo_codes_g[:], xo_w[:].bitcast(U32).indirect(idx2[:]))
+        w2_d = deal(nc.scalar.copy, w2_w, U16, "w2_d")
+        b_accs = []
+        for t in range(PACK):
+            acc = psum.tile([P, J], F32, name=f"b_acc{t}", tag=f"first{t}")
+            first_product(acc[:], w2_d, w2_plane_d, xo_codes_g[:], xo_scales_g[:], t)
+            b_accs.append(acc)
+
+        x1 = held.tile([P, PACK, J], BF16, name="x1")
+        woven = [held.tile([P, HALF, PACK], BF16, name=f"x1_woven{h}", tag=f"x1_woven{h}", align_bytes=ALIGN) for h in range(2)]
+
+        def look_up_codes(t):
+            nc.scalar.activation(out=x1[:, t, :], in_=cq_t[t][:].indirect(idx[:]), func=COPY, scale=gs_t[:, t : t + 1])
+
+        def weave(h, first):
+            nc.vector.tensor_copy(
+                woven[h][:, :, first : first + 2].rearrange("p (c i) t -> p c t i", i=2),
+                x1[:, first : first + 2, HALF * h : HALF * (h + 1)].rearrange("p t (c i) -> p c t i", i=2),
+            )
+
+        def looked_tile(name, tag=""):
+            return held.tile([P, 2, 2, HALF], F32, name=name, tag=tag or name)
+
+        look_up_codes(0)
+        look_up_codes(1)
+        b_rows = [rows_of(nc.vector.tensor_copy, b_accs[t], f"b_rows{t}") for t in range(PACK)]
+        looked = looked_tile("b_looked0")
+        for t in range(2):
+            look_up_gated(looked, b_rows[t], t, idx5, sb_t, idx6, sh_t, bh_t)
+        weave(0, 0)
+        weave(1, 0)
+        spread(w_plane, w_staged)
+        w_plane_d = deal(nc.vector.tensor_copy, w_plane, U8, "w_plane_d")
+        w_d = deal(nc.vector.tensor_copy, w_w, U16, "w_d")
+        late_hid = held.tile([P, HALF, PACK], BF16, name="late_hid", align_bytes=ALIGN)
+        gate(late_hid, looked, 0)
+        look_up_codes(2)
+        look_up_codes(3)
+
+        x1_codes = held.tile([P, J], U32, name="x1_codes", align_bytes=ALIGN)
+        x1_scales = held.tile([P, J], U8, name="x1_scales", align_bytes=ALIGN)
+        halves = [slice(HALF * h, HALF * (h + 1)) for h in range(2)]
+        weave(0, 2)
+        weave(1, 2)
+        for h in range(2):
+            quantise(woven[h], x1_codes[:, halves[h]], x1_scales[:, halves[h]])
+        looked = looked_tile("b_looked1", "cq3")
+        for t in range(2, PACK):
+            look_up_gated(looked, b_rows[t], t, idx5, sb_t, idx6, sh_t, bh_t)
+
+        a_accs = []
+        for t in range(PACK):
+            acc = psum.tile([P, J], F32, name=f"a_acc{t}", tag=f"first{t}")
+            if t == 0:
+                for h in range(2):
+                    first_product(acc[:, halves[h]], w_d, w_plane_d, x1_codes[:, halves[h]], x1_scales[:, halves[h]], t)
+            else:
+                first_product(acc[:], w_d, w_plane_d, x1_codes[:], x1_scales[:], t)
+            a_accs.append(acc)
+
+        last_plane = zeroed_plane(3 * N, "last_plane", "x1_woven1")
+        spread(last_plane, last_staged[:].rearrange("r q i c -> r q (i c)"))
+        gate(late_hid, looked, 2)
+        a_rows = [rows_of(nc.scalar.copy, a_accs[0], "a_rows0")]
+        a_rows.append(rows_of(nc.vector.tensor_copy, a_accs[1], "a_rows1"))
+        late_q = quantise_hid(late_hid, "late")
+        a_rows.extend(rows_of(nc.vector.tensor_copy, a_accs[t], f"a_rows{t}") for t in (2, 3))
+
+        sums = {}
+        for h in (1, 0):
+            for n in range(2):
+                acc = psum.tile([P, HALF], F32, name=f"p_acc{h}{n}", tag=f"p_acc{h}{n}")
+                nc.tensor.matmul_mx(
+                    out=acc[:],
+                    lhsT=ws_w[:, 2 * P * n : 2 * P * (n + 1)].bitcast(FP4X4),
+                    lhsT_scale=last_plane[:, N + P * n : N + P * (n + 1)],
+                    rhs=sx_w[:, 4 * HALF * h : 4 * HALF * (h + 1)].bitcast(FP8X4),
+                    rhs_scale=last_plane[:, 2 * N + HALF * h : 2 * N + HALF * (h + 1)],
+                    start=True,
+                    stop=False,
+                )
+                sums[h, n] = acc
+
+        def second_stage(h, codes, scales):
+            for n in range(2):
+                nc.tensor.matmul_mx(
+                    out=sums[h, n][:],
+                    lhsT=wb_w[:, 2 * P * n : 2 * P * (n + 1)].bitcast(FP4X4),
+                    lhsT_scale=last_plane[:, P * n : P * (n + 1)],
+                    rhs=codes[:].bitcast(FP8X4),
+                    rhs_scale=scales[:],
+                    start=False,
+                    stop=True,
+                )
+
+        def place(h, n, tag=""):
+            name = f"p_values{h}{n}"
+            values = held.tile([P, HALF], F32, name=name, tag=tag or name)
+            window = pages[n][:].indirect(idx7[:, 8 * h : 8 * (h + 1)])
+            if n == 0:
+                nc.vector.tensor_copy(values[:], sums[h, n][:])
+                nc.vector.tensor_copy(window, values[:])
+            else:
+                nc.scalar.copy(values[:], sums[h, n][:])
+                nc.scalar.activation(out=window, in_=values[:], func=COPY)
+
+        second_stage(1, *late_q)
+        looked = looked_tile("a_looked0")
+        hid = held.tile([P, HALF, PACK], BF16, name="hid", align_bytes=ALIGN)
+        for t in range(2):
+            look_up_gated(looked, a_rows[t], t, idx3, sa_t, idx4, sg_t, bg_t)
+        gate(hid, looked, 0)
+        place(1, 0)
+        looked = looked_tile("a_looked1")
+        for t in range(2, PACK):
+            look_up_gated(looked, a_rows[t], t, idx3, sa_t, idx4, sg_t, bg_t)
+        gate(hid, looked, 2)
+        place(1, 1, "a_rows3")
+        second_stage(0, *quantise_hid(hid, "early"))
+        place(0, 0)
+        place(0, 1)
+        for n in range(2):
+            nc.sync.dma_start(out[P * n : P * (n + 1), :], pages[n][:])

@@ -75,11 +75,6 @@ def tile_list_gatedsides_codednote_further_scattered_kernel(
             )
             return tile
 
-        warm_in = held.tile([P, 1], F32, name="warm_in")
-        warm_out = held.tile([P, 1], F32, name="warm_out")
-        nc.vector.memset(warm_in[:], 0.0)
-        nc.scalar.activation(out=warm_out[:], in_=warm_in[:], func=SIGMOID)
-
         def zeroed_page(name):
             page = held.tile([P, E], F32, name=name)
             nc.vector.memset(page[:].bitcast(I32), 0)

@@ -75,6 +75,11 @@ def tile_list_gatedsides_codednote_further_scattered_kernel(
             )
             return tile
 
+        warm_in = held.tile([P, 1], F32, name="warm_in")
+        warm_out = held.tile([P, 1], F32, name="warm_out")
+        nc.vector.memset(warm_in[:], 0.0)
+        nc.scalar.activation(out=warm_out[:], in_=warm_in[:], func=SIGMOID)
+
         def zeroed_page(name):
             page = held.tile([P, E], F32, name=name)
             nc.vector.memset(page[:].bitcast(I32), 0)
@@ -100,24 +105,25 @@ def tile_list_gatedsides_codednote_further_scattered_kernel(
         idx = load_list(offs, "idx")
         gs_t = load_per_row(nc.sync, gs, "gs_t")
         cq_t = [load_cq(0), load_cq(1)]
+        idx6 = load_list(offs6, "idx6")
+        sh_t = load_per_row(nc.sync, sh, "sh_t")
+        bh_t = load_per_row(nc.sync, bh, "bh_t")
+        idx5 = load_list(offs5, "idx5")
+        sb_t = load_per_row(nc.sync, sb, "sb_t")
+        cq_t.append(load_cq(2))
         w_staged = stage_scales(nc.sync, w_scales, "w_staged")
         w_w = load_bytes(w_words[0], "w_w")
-        idx6 = load_list(offs6, "idx6")
-        idx5 = load_list(offs5, "idx5")
-        cq_t.extend([load_cq(2), load_cq(3)])
+        cq_t.append(load_cq(3))
         last_staged = held.tile([4, QUADS, 3, N // 4], I32, name="last_staged")
         for i, src in enumerate((wb_scales, ws_scales, sx_scales)):
             nc.sync.dma_start(last_staged[:, :, i, :], scale_rows(src))
+        idx4 = load_list(offs4, "idx4")
+        idx3 = load_list(offs3, "idx3")
         ws_w = load_bytes(ws_words[0], "ws_w")
         sx_w = load_bytes(sx_words[0].rearrange("p d t -> p (d t)"), "sx_w")
         wb_w = load_bytes(wb_words[0], "wb_w")
-        idx4 = load_list(offs4, "idx4")
-        idx3 = load_list(offs3, "idx3")
         idx7 = load_list(offs7, "idx7")
 
-        sh_t = load_per_row(nc.gpsimd, sh, "sh_t")
-        bh_t = load_per_row(nc.gpsimd, bh, "bh_t")
-        sb_t = load_per_row(nc.gpsimd, sb, "sb_t")
         sg_t = load_per_row(nc.gpsimd, sg, "sg_t")
         bg_t = load_per_row(nc.gpsimd, bg, "bg_t")
         sa_t = load_per_row(nc.gpsimd, sa, "sa_t")
@@ -140,16 +146,16 @@ def tile_list_gatedsides_codednote_further_scattered_kernel(
 
         def look_up_gated(looked, rows, t, value_idx, weight, gate_idx, slope, offset):
             nc.scalar.activation(
-                out=looked[:, 0, t % 2, :], in_=rows[:].indirect(gate_idx[:]), func=SIGMOID,
+                out=looked[:, 0, t % looked.shape[2], :], in_=rows[:].indirect(gate_idx[:]), func=SIGMOID,
                 bias=offset[:, t : t + 1], scale=slope[:, t : t + 1],
             )
             nc.scalar.activation(
-                out=looked[:, 1, t % 2, :], in_=rows[:].indirect(value_idx[:]), func=COPY, scale=weight[:, t : t + 1],
+                out=looked[:, 1, t % looked.shape[2], :], in_=rows[:].indirect(value_idx[:]), func=COPY, scale=weight[:, t : t + 1],
             )
 
         def gate(hid, looked, first):
             nc.vector.tensor_tensor(
-                hid[:, :, first : first + 2].rearrange("p (c i) t -> p c t i", i=2),
+                hid[:, :, first : first + looked.shape[2]].rearrange("p (c i) t -> p c t i", i=2),
                 looked[:, 1, :, :].rearrange("p t (c i) -> p c t i", i=2),
                 looked[:, 0, :, :].rearrange("p t (c i) -> p c t i", i=2),
                 MULT,
@@ -204,7 +210,7 @@ def tile_list_gatedsides_codednote_further_scattered_kernel(
         spread(w_plane, w_staged)
         w_plane_d = deal(nc.vector.tensor_copy, w_plane, U8, "w_plane_d")
         w_d = deal(nc.vector.tensor_copy, w_w, U16, "w_d")
-        late_hid = held.tile([P, HALF, PACK], BF16, name="late_hid", align_bytes=ALIGN)
+        late_hid = held.tile([P, HALF, PACK], BF16, name="late_hid", tag="w_w", align_bytes=ALIGN)
         gate(late_hid, looked, 0)
         look_up_codes(2)
         look_up_codes(3)
@@ -265,31 +271,30 @@ def tile_list_gatedsides_codednote_further_scattered_kernel(
                     stop=True,
                 )
 
-        def place(h, n, tag=""):
+        def out_of_psum(h, n, tag="", align=None):
             name = f"p_values{h}{n}"
-            values = held.tile([P, HALF], F32, name=name, tag=tag or name)
+            values = held.tile([P, HALF], F32, name=name, tag=tag or name, align_bytes=align)
+            copy = nc.vector.tensor_copy if n == 0 else nc.scalar.copy
+            copy(values[:], sums[h, n][:])
+            return values
+
+        def place(values, h, n):
             window = pages[n][:].indirect(idx7[:, 8 * h : 8 * (h + 1)])
             if n == 0:
-                nc.vector.tensor_copy(values[:], sums[h, n][:])
                 nc.vector.tensor_copy(window, values[:])
             else:
-                nc.scalar.copy(values[:], sums[h, n][:])
                 nc.scalar.activation(out=window, in_=values[:], func=COPY)
 
         second_stage(1, *late_q)
-        looked = looked_tile("a_looked0")
-        hid = held.tile([P, HALF, PACK], BF16, name="hid", align_bytes=ALIGN)
-        for t in range(2):
+        place(out_of_psum(1, 0, "late_values", ALIGN), 1, 0)
+        looked = held.tile([P, 2, PACK, HALF], F32, name="a_looked")
+        for t in range(PACK):
             look_up_gated(looked, a_rows[t], t, idx3, sa_t, idx4, sg_t, bg_t)
+        hid = held.tile([P, HALF, PACK], BF16, name="hid", tag="late_values", align_bytes=ALIGN)
         gate(hid, looked, 0)
-        place(1, 0)
-        looked = looked_tile("a_looked1")
-        for t in range(2, PACK):
-            look_up_gated(looked, a_rows[t], t, idx3, sa_t, idx4, sg_t, bg_t)
-        gate(hid, looked, 2)
-        place(1, 1, "a_rows3")
-        second_stage(0, *quantise_hid(hid, "early"))
-        place(0, 0)
-        place(0, 1)
+        early_q = quantise_hid(hid, "early")
+        place(out_of_psum(1, 1, "a_rows3"), 1, 1)
+        second_stage(0, *early_q)
         for n in range(2):
+            place(out_of_psum(0, n), 0, n)
             nc.sync.dma_start(out[P * n : P * (n + 1), :], pages[n][:])

@@ -21,6 +21,7 @@ P = 128
 PACK = 4
 QUADS = 4
 ALIGN = 64
+W2_AT, W_AT, WB_AT, WS_AT, SX_AT, PLANES_WIDTH = 0, R, 2 * R, 2 * R + N, 2 * R + 2 * N, 2 * R + 2 * N + D
 
 
 def tile_list_gatedsides_codednote_further_scattered_kernel(
@@ -43,21 +44,16 @@ def tile_list_gatedsides_codednote_further_scattered_kernel(
             nc.sync.dma_start(tile[:].bitcast(I32), src.bitcast(I32))
             return tile
 
-        def load_per_row(queue, src, name):
+        def load_per_row(src, name):
             tile = held.tile([P, PACK], F32, name=name)
-            queue.dma_start(tile[:], src.rearrange("(p t) o -> p (t o)", t=PACK))
+            nc.sync.dma_start(tile[:], src.rearrange("(p t) o -> p (t o)", t=PACK))
             return tile
 
         def scale_rows(src):
             return src[0].bitcast(I32).rearrange("(q r) c -> r q c", r=4)
 
-        def stage_scales(queue, src, name):
-            tile = held.tile([4, QUADS, src.shape[2] // 4], I32, name=name)
-            queue.dma_start(tile[:], scale_rows(src))
-            return tile
-
-        def zeroed_plane(width, name, tag=""):
-            tile = held.tile([P, width], U8, name=name, tag=tag or name, align_bytes=ALIGN)
+        def zeroed_plane(width, name):
+            tile = held.tile([P, width], U8, name=name, align_bytes=ALIGN)
             nc.vector.memset(tile[:].bitcast(I32), 0)
             return tile
 
@@ -66,12 +62,10 @@ def tile_list_gatedsides_codednote_further_scattered_kernel(
                 nc.vector.tensor_copy(plane[32 * q : 32 * q + 4, :].bitcast(I32), staged[:, q, :])
 
         def deal(copy, src, dtype, name):
-            tile = held.tile(list(src.shape), U8, name=name, tag=name, align_bytes=ALIGN)
-            src_v, dst_v = src[:], tile[:]
-            if dtype is not U8:
-                src_v, dst_v = src_v.bitcast(dtype), dst_v.bitcast(dtype)
+            tile = held.tile([P, 2 * R], U8, name=name, align_bytes=ALIGN)
             copy(
-                dst_v.rearrange("p (t m) -> p t m", t=PACK), src_v.rearrange("p (m t) -> p t m", t=PACK)
+                tile[:].bitcast(dtype).rearrange("p (i t m) -> p i t m", t=PACK, m=P),
+                src.bitcast(dtype).rearrange("p (i m t) -> p i t m", t=PACK, m=P),
             )
             return tile
 
@@ -82,12 +76,11 @@ def tile_list_gatedsides_codednote_further_scattered_kernel(
 
         def zeroed_page(name):
             page = held.tile([P, E], F32, name=name)
-            nc.vector.memset(page[:].bitcast(I32), 0)
+            nc.gpsimd.memset(page[:], 0.0)
             return page
 
         xo_plane = zeroed_plane(Z, "xo_plane")
-        w2_plane = zeroed_plane(R, "w2_plane")
-        w_plane = zeroed_plane(R, "w_plane")
+        weight_planes = zeroed_plane(PLANES_WIDTH, "weight_planes")
         pages = [zeroed_page(f"page{n}") for n in range(2)]
 
         cq_rows = cq.rearrange("(p t) c -> t p c", t=PACK)
@@ -98,35 +91,32 @@ def tile_list_gatedsides_codednote_further_scattered_kernel(
             return tile
 
         idx2 = load_list(offs2, "idx2")
-        xo_staged = stage_scales(nc.sync, xo_scales, "xo_staged")
-        w2_staged = stage_scales(nc.sync, w2_scales, "w2_staged")
-        w2_w = load_bytes(w2_words[0], "w2_w")
+        xo_staged = held.tile([4, QUADS, Z // 4], I32, name="xo_staged")
+        nc.sync.dma_start(xo_staged[:], scale_rows(xo_scales))
+        weights_staged = held.tile([4, QUADS, PLANES_WIDTH // 4], I32, name="weights_staged")
+        for at, src in ((W2_AT, w2_scales), (W_AT, w_scales), (WB_AT, wb_scales), (WS_AT, ws_scales), (SX_AT, sx_scales)):
+            nc.sync.dma_start(weights_staged[:, :, at // 4 : (at + src.shape[2]) // 4], scale_rows(src))
         xo_w = load_bytes(xo_words[0].rearrange("p z t -> p (z t)"), "xo_w")
         idx = load_list(offs, "idx")
-        gs_t = load_per_row(nc.sync, gs, "gs_t")
+        gs_t = load_per_row(gs, "gs_t")
+        w2_w = load_bytes(w2_words[0], "w2_w")
+        w_w = load_bytes(w_words[0], "w_w")
         cq_t = [load_cq(0), load_cq(1)]
         idx6 = load_list(offs6, "idx6")
-        sh_t = load_per_row(nc.sync, sh, "sh_t")
-        bh_t = load_per_row(nc.sync, bh, "bh_t")
+        sh_t = load_per_row(sh, "sh_t")
+        bh_t = load_per_row(bh, "bh_t")
         idx5 = load_list(offs5, "idx5")
-        sb_t = load_per_row(nc.sync, sb, "sb_t")
-        cq_t.append(load_cq(2))
-        w_staged = stage_scales(nc.sync, w_scales, "w_staged")
-        w_w = load_bytes(w_words[0], "w_w")
-        cq_t.append(load_cq(3))
-        last_staged = held.tile([4, QUADS, 3, N // 4], I32, name="last_staged")
-        for i, src in enumerate((wb_scales, ws_scales, sx_scales)):
-            nc.sync.dma_start(last_staged[:, :, i, :], scale_rows(src))
+        sb_t = load_per_row(sb, "sb_t")
+        cq_t.extend([load_cq(2), load_cq(3)])
         idx4 = load_list(offs4, "idx4")
+        sg_t = load_per_row(sg, "sg_t")
+        bg_t = load_per_row(bg, "bg_t")
         idx3 = load_list(offs3, "idx3")
+        sa_t = load_per_row(sa, "sa_t")
         ws_w = load_bytes(ws_words[0], "ws_w")
         sx_w = load_bytes(sx_words[0].rearrange("p d t -> p (d t)"), "sx_w")
         wb_w = load_bytes(wb_words[0], "wb_w")
         idx7 = load_list(offs7, "idx7")
-
-        sg_t = load_per_row(nc.gpsimd, sg, "sg_t")
-        bg_t = load_per_row(nc.gpsimd, bg, "bg_t")
-        sa_t = load_per_row(nc.gpsimd, sa, "sa_t")
 
         def first_product(acc, words, plane, codes, scales, t):
             nc.tensor.matmul_mx(
@@ -146,18 +136,18 @@ def tile_list_gatedsides_codednote_further_scattered_kernel(
 
         def look_up_gated(looked, rows, t, value_idx, weight, gate_idx, slope, offset):
             nc.scalar.activation(
-                out=looked[:, 0, t % looked.shape[2], :], in_=rows[:].indirect(gate_idx[:]), func=SIGMOID,
+                out=looked[:, 0, t % 2, :], in_=rows[:].indirect(gate_idx[:]), func=SIGMOID,
                 bias=offset[:, t : t + 1], scale=slope[:, t : t + 1],
             )
             nc.scalar.activation(
-                out=looked[:, 1, t % looked.shape[2], :], in_=rows[:].indirect(value_idx[:]), func=COPY, scale=weight[:, t : t + 1],
+                out=looked[:, 1, t % 2, :], in_=rows[:].indirect(value_idx[:]), func=COPY, scale=weight[:, t : t + 1],
             )
 
         def gate(hid, looked, first):
             nc.vector.tensor_tensor(
-                hid[:, :, first : first + looked.shape[2]].rearrange("p (c i) t -> p c t i", i=2),
-                looked[:, 1, :, :].rearrange("p t (c i) -> p c t i", i=2),
-                looked[:, 0, :, :].rearrange("p t (c i) -> p c t i", i=2),
+                hid[:, :, first : first + 2].rearrange("p (c i) t -> p c t i", i=4),
+                looked[:, 1, :, :].rearrange("p t (c i) -> p c t i", i=4),
+                looked[:, 0, :, :].rearrange("p t (c i) -> p c t i", i=4),
                 MULT,
             )
 
@@ -173,11 +163,13 @@ def tile_list_gatedsides_codednote_further_scattered_kernel(
         spread(xo_plane, xo_staged)
         xo_scales_g = held.tile([P, J], U8, name="xo_scales_g", align_bytes=ALIGN)
         nc.vector.tensor_copy(xo_scales_g[:], xo_plane[:].indirect(idx2[:]))
-        spread(w2_plane, w2_staged)
-        w2_plane_d = deal(nc.vector.tensor_copy, w2_plane, U8, "w2_plane_d")
+        spread(weight_planes, weights_staged)
+        dealt_planes = deal(nc.vector.tensor_copy, weight_planes[:, W2_AT:WB_AT], U8, "dealt_planes")
+        w2_plane_d, w_plane_d = dealt_planes[:, W2_AT:W_AT], dealt_planes[:, W_AT:WB_AT]
         xo_codes_g = held.tile([P, J], U32, name="xo_codes_g", align_bytes=ALIGN)
         nc.vector.tensor_copy(xo_codes_g[:], xo_w[:].bitcast(U32).indirect(idx2[:]))
-        w2_d = deal(nc.scalar.copy, w2_w, U16, "w2_d")
+        w2_d = deal(nc.scalar.copy, w2_w[:], U16, "w2_d")
+        w_d = deal(nc.scalar.copy, w_w[:], U16, "w_d")
         b_accs = []
         for t in range(PACK):
             acc = psum.tile([P, J], F32, name=f"b_acc{t}", tag=f"first{t}")
@@ -192,8 +184,8 @@ def tile_list_gatedsides_codednote_further_scattered_kernel(
 
         def weave(h, first):
             nc.vector.tensor_copy(
-                woven[h][:, :, first : first + 2].rearrange("p (c i) t -> p c t i", i=2),
-                x1[:, first : first + 2, HALF * h : HALF * (h + 1)].rearrange("p t (c i) -> p c t i", i=2),
+                woven[h][:, :, first : first + 2].rearrange("p (c i) t -> p c t i", i=4),
+                x1[:, first : first + 2, HALF * h : HALF * (h + 1)].rearrange("p t (c i) -> p c t i", i=4),
             )
 
         def looked_tile(name, tag=""):
@@ -207,10 +199,7 @@ def tile_list_gatedsides_codednote_further_scattered_kernel(
             look_up_gated(looked, b_rows[t], t, idx5, sb_t, idx6, sh_t, bh_t)
         weave(0, 0)
         weave(1, 0)
-        spread(w_plane, w_staged)
-        w_plane_d = deal(nc.vector.tensor_copy, w_plane, U8, "w_plane_d")
-        w_d = deal(nc.vector.tensor_copy, w_w, U16, "w_d")
-        late_hid = held.tile([P, HALF, PACK], BF16, name="late_hid", tag="w_w", align_bytes=ALIGN)
+        late_hid = held.tile([P, HALF, PACK], BF16, name="late_hid", align_bytes=ALIGN)
         gate(late_hid, looked, 0)
         look_up_codes(2)
         look_up_codes(3)
@@ -236,8 +225,6 @@ def tile_list_gatedsides_codednote_further_scattered_kernel(
                 first_product(acc[:], w_d, w_plane_d, x1_codes[:], x1_scales[:], t)
             a_accs.append(acc)
 
-        last_plane = zeroed_plane(3 * N, "last_plane", "x1_woven1")
-        spread(last_plane, last_staged[:].rearrange("r q i c -> r q (i c)"))
         gate(late_hid, looked, 2)
         a_rows = [rows_of(nc.scalar.copy, a_accs[0], "a_rows0")]
         a_rows.append(rows_of(nc.vector.tensor_copy, a_accs[1], "a_rows1"))
@@ -251,9 +238,9 @@ def tile_list_gatedsides_codednote_further_scattered_kernel(
                 nc.tensor.matmul_mx(
                     out=acc[:],
                     lhsT=ws_w[:, 2 * P * n : 2 * P * (n + 1)].bitcast(FP4X4),
-                    lhsT_scale=last_plane[:, N + P * n : N + P * (n + 1)],
+                    lhsT_scale=weight_planes[:, WS_AT + P * n : WS_AT + P * (n + 1)],
                     rhs=sx_w[:, 4 * HALF * h : 4 * HALF * (h + 1)].bitcast(FP8X4),
-                    rhs_scale=last_plane[:, 2 * N + HALF * h : 2 * N + HALF * (h + 1)],
+                    rhs_scale=weight_planes[:, SX_AT + HALF * h : SX_AT + HALF * (h + 1)],
                     start=True,
                     stop=False,
                 )
@@ -264,7 +251,7 @@ def tile_list_gatedsides_codednote_further_scattered_kernel(
                 nc.tensor.matmul_mx(
                     out=sums[h, n][:],
                     lhsT=wb_w[:, 2 * P * n : 2 * P * (n + 1)].bitcast(FP4X4),
-                    lhsT_scale=last_plane[:, P * n : P * (n + 1)],
+                    lhsT_scale=weight_planes[:, WB_AT + P * n : WB_AT + P * (n + 1)],
                     rhs=codes[:].bitcast(FP8X4),
                     rhs_scale=scales[:],
                     start=False,
@@ -287,14 +274,16 @@ def tile_list_gatedsides_codednote_further_scattered_kernel(
 
         second_stage(1, *late_q)
         place(out_of_psum(1, 0, "late_values", ALIGN), 1, 0)
-        looked = held.tile([P, 2, PACK, HALF], F32, name="a_looked")
-        for t in range(PACK):
-            look_up_gated(looked, a_rows[t], t, idx3, sa_t, idx4, sg_t, bg_t)
         hid = held.tile([P, HALF, PACK], BF16, name="hid", tag="late_values", align_bytes=ALIGN)
-        gate(hid, looked, 0)
+        for pair in range(2):
+            looked = looked_tile(f"a_looked{pair}")
+            for t in range(2 * pair, 2 * pair + 2):
+                look_up_gated(looked, a_rows[t], t, idx3, sa_t, idx4, sg_t, bg_t)
+            gate(hid, looked, 2 * pair)
         early_q = quantise_hid(hid, "early")
         place(out_of_psum(1, 1, "a_rows3"), 1, 1)
         second_stage(0, *early_q)
         for n in range(2):
             place(out_of_psum(0, n), 0, n)
-            nc.sync.dma_start(out[P * n : P * (n + 1), :], pages[n][:])
+            queue = nc.sync if n == 0 else nc.scalar
+            queue.dma_start(out[P * n : P * (n + 1), :], pages[n][:])

from contextlib import ExitStack

import concourse.mybir as mybir

K, T, J, R, Z, HALF, D, N, E = 512, 1024, 256, 512, 1024, 128, 256, 256, 1024
FLOPS = 2 * (K * R * J + K * R * J + R * N * D + K * N * D)

F32 = mybir.dt.float32
BF16 = mybir.dt.bfloat16
I32 = mybir.dt.int32
U32 = mybir.dt.uint32
U16 = mybir.dt.uint16
U8 = mybir.dt.uint8
FP8X4 = mybir.dt.float8_e4m3fn_x4
FP4X4 = mybir.dt.float4_e2m1fn_x4
COPY = mybir.ActivationFunctionType.Copy
SIGMOID = mybir.ActivationFunctionType.Sigmoid
MULT = mybir.AluOpType.mult

P = 128
PACK = 4
QUADS = 4
ALIGN = 64
W2_AT, W_AT, WB_AT, WS_AT, SX_AT, PLANES_WIDTH = 0, R, 2 * R, 2 * R + N, 2 * R + 2 * N, 2 * R + 2 * N + D


def tile_list_gatedsides_codednote_further_scattered_kernel(
    tc, xo_words, xo_scales, cq, gs, w_words, w_scales, w2_words, w2_scales, sa, sb, sg, bg, sh, bh,
    wb_words, wb_scales, sx_words, sx_scales, ws_words, ws_scales,
    offs, offs2, offs3, offs4, offs5, offs6, offs7, out,
):
    nc = tc.nc
    with ExitStack() as ctx:
        held = ctx.enter_context(tc.tile_pool(name="held", bufs=1))
        psum = ctx.enter_context(tc.psum_pool(name="psum", bufs=1))

        def load_list(src, name):
            tile = held.tile(list(src.shape), U16, name=name)
            nc.sync.dma_start(tile[:], src)
            return tile

        def load_bytes(src, name):
            tile = held.tile(list(src.shape), U8, name=name, tag=name, align_bytes=ALIGN)
            nc.sync.dma_start(tile[:].bitcast(I32), src.bitcast(I32))
            return tile

        def load_per_row(src, name):
            tile = held.tile([P, PACK], F32, name=name)
            nc.sync.dma_start(tile[:], src.rearrange("(p t) o -> p (t o)", t=PACK))
            return tile

        def scale_rows(src):
            return src[0].bitcast(I32).rearrange("(q r) c -> r q c", r=4)

        def zeroed_plane(width, name):
            tile = held.tile([P, width], U8, name=name, align_bytes=ALIGN)
            nc.vector.memset(tile[:].bitcast(I32), 0)
            return tile

        def spread(plane, staged):
            for q in range(QUADS):
                nc.vector.tensor_copy(plane[32 * q : 32 * q + 4, :].bitcast(I32), staged[:, q, :])

        def deal(copy, src, dtype, name):
            tile = held.tile([P, 2 * R], U8, name=name, align_bytes=ALIGN)
            copy(
                tile[:].bitcast(dtype).rearrange("p (i t m) -> p i t m", t=PACK, m=P),
                src.bitcast(dtype).rearrange("p (i m t) -> p i t m", t=PACK, m=P),
            )
            return tile

        warm_in = held.tile([P, 1], F32, name="warm_in")
        warm_out = held.tile([P, 1], F32, name="warm_out")
        nc.vector.memset(warm_in[:], 0.0)
        nc.scalar.activation(out=warm_out[:], in_=warm_in[:], func=SIGMOID)

        def zeroed_page(name):
            page = held.tile([P, E], F32, name=name)
            nc.gpsimd.memset(page[:], 0.0)
            return page

        xo_plane = zeroed_plane(Z, "xo_plane")
        weight_planes = zeroed_plane(PLANES_WIDTH, "weight_planes")
        pages = [zeroed_page(f"page{n}") for n in range(2)]

        cq_rows = cq.rearrange("(p t) c -> t p c", t=PACK)

        def load_cq(t):
            tile = held.tile([P, T], F32, name=f"cq{t}", tag=f"cq{t}")
            nc.sync.dma_start(tile[:], cq_rows[t])
            return tile

        idx2 = load_list(offs2, "idx2")
        xo_staged = held.tile([4, QUADS, Z // 4], I32, name="xo_staged")
        nc.sync.dma_start(xo_staged[:], scale_rows(xo_scales))
        weights_staged = held.tile([4, QUADS, PLANES_WIDTH // 4], I32, name="weights_staged")
        for at, src in ((W2_AT, w2_scales), (W_AT, w_scales), (WB_AT, wb_scales), (WS_AT, ws_scales), (SX_AT, sx_scales)):
            nc.sync.dma_start(weights_staged[:, :, at // 4 : (at + src.shape[2]) // 4], scale_rows(src))
        xo_w = load_bytes(xo_words[0].rearrange("p z t -> p (z t)"), "xo_w")
        idx = load_list(offs, "idx")
        gs_t = load_per_row(gs, "gs_t")
        w2_w = load_bytes(w2_words[0], "w2_w")
        w_w = load_bytes(w_words[0], "w_w")
        cq_t = [load_cq(0), load_cq(1)]
        idx6 = load_list(offs6, "idx6")
        sh_t = load_per_row(sh, "sh_t")
        bh_t = load_per_row(bh, "bh_t")
        idx5 = load_list(offs5, "idx5")
        sb_t = load_per_row(sb, "sb_t")
        cq_t.extend([load_cq(2), load_cq(3)])
        idx4 = load_list(offs4, "idx4")
        sg_t = load_per_row(sg, "sg_t")
        bg_t = load_per_row(bg, "bg_t")
        idx3 = load_list(offs3, "idx3")
        sa_t = load_per_row(sa, "sa_t")
        ws_w = load_bytes(ws_words[0], "ws_w")
        sx_w = load_bytes(sx_words[0].rearrange("p d t -> p (d t)"), "sx_w")
        wb_w = load_bytes(wb_words[0], "wb_w")
        idx7 = load_list(offs7, "idx7")

        def first_product(acc, words, plane, codes, scales, t):
            nc.tensor.matmul_mx(
                out=acc,
                lhsT=words[:, 2 * P * t : 2 * P * (t + 1)].bitcast(FP4X4),
                lhsT_scale=plane[:, P * t : P * (t + 1)],
                rhs=codes.bitcast(FP8X4),
                rhs_scale=scales,
                start=True,
                stop=True,
            )

        def rows_of(copy, acc, name, tag=""):
            tile = held.tile([P, J], F32, name=name, tag=tag or name)
            copy(tile[:], acc[:])
            return tile

        def look_up_gated(looked, rows, t, value_idx, weight, gate_idx, slope, offset):
            nc.scalar.activation(
                out=looked[:, 0, t % 2, :], in_=rows[:].indirect(gate_idx[:]), func=SIGMOID,
                bias=offset[:, t : t + 1], scale=slope[:, t : t + 1],
            )
            nc.scalar.activation(
                out=looked[:, 1, t % 2, :], in_=rows[:].indirect(value_idx[:]), func=COPY, scale=weight[:, t : t + 1],
            )

        def gate(hid, looked, first):
            nc.vector.tensor_tensor(
                hid[:, :, first : first + 2].rearrange("p (c i) t -> p c t i", i=4),
                looked[:, 1, :, :].rearrange("p t (c i) -> p c t i", i=4),
                looked[:, 0, :, :].rearrange("p t (c i) -> p c t i", i=4),
                MULT,
            )

        def quantise(src, codes, scales):
            nc.vector.quantize_mx(out=codes.bitcast(FP8X4), scales=scales, in_=src[:].rearrange("p c t -> p (c t)"))

        def quantise_hid(hid, name):
            codes = held.tile([P, HALF], U32, name=f"{name}_codes", align_bytes=ALIGN)
            scales = held.tile([P, HALF], U8, name=f"{name}_scales", align_bytes=ALIGN)
            quantise(hid, codes[:], scales[:])
            return codes, scales

        spread(xo_plane, xo_staged)
        xo_scales_g = held.tile([P, J], U8, name="xo_scales_g", align_bytes=ALIGN)
        nc.vector.tensor_copy(xo_scales_g[:], xo_plane[:].indirect(idx2[:]))
        spread(weight_planes, weights_staged)
        dealt_planes = deal(nc.vector.tensor_copy, weight_planes[:, W2_AT:WB_AT], U8, "dealt_planes")
        w2_plane_d, w_plane_d = dealt_planes[:, W2_AT:W_AT], dealt_planes[:, W_AT:WB_AT]
        xo_codes_g = held.tile([P, J], U32, name="xo_codes_g", align_bytes=ALIGN)
        nc.vector.tensor_copy(xo_codes_g[:], xo_w[:].bitcast(U32).indirect(idx2[:]))
        w2_d = deal(nc.scalar.copy, w2_w[:], U16, "w2_d")
        w_d = deal(nc.scalar.copy, w_w[:], U16, "w_d")
        b_accs = []
        for t in range(PACK):
            acc = psum.tile([P, J], F32, name=f"b_acc{t}", tag=f"first{t}")
            first_product(acc[:], w2_d, w2_plane_d, xo_codes_g[:], xo_scales_g[:], t)
            b_accs.append(acc)

        x1 = held.tile([P, PACK, J], BF16, name="x1")
        woven = [held.tile([P, HALF, PACK], BF16, name=f"x1_woven{h}", tag=f"x1_woven{h}", align_bytes=ALIGN) for h in range(2)]

        def look_up_codes(t):
            nc.scalar.activation(out=x1[:, t, :], in_=cq_t[t][:].indirect(idx[:]), func=COPY, scale=gs_t[:, t : t + 1])

        def weave(h, first):
            nc.vector.tensor_copy(
                woven[h][:, :, first : first + 2].rearrange("p (c i) t -> p c t i", i=4),
                x1[:, first : first + 2, HALF * h : HALF * (h + 1)].rearrange("p t (c i) -> p c t i", i=4),
            )

        def looked_tile(name, tag=""):
            return held.tile([P, 2, 2, HALF], F32, name=name, tag=tag or name)

        look_up_codes(0)
        look_up_codes(1)
        b_rows = [rows_of(nc.vector.tensor_copy, b_accs[t], f"b_rows{t}") for t in range(PACK)]
        looked = looked_tile("b_looked0")
        for t in range(2):
            look_up_gated(looked, b_rows[t], t, idx5, sb_t, idx6, sh_t, bh_t)
        weave(0, 0)
        weave(1, 0)
        late_hid = held.tile([P, HALF, PACK], BF16, name="late_hid", align_bytes=ALIGN)
        gate(late_hid, looked, 0)
        look_up_codes(2)
        look_up_codes(3)

        x1_codes = held.tile([P, J], U32, name="x1_codes", align_bytes=ALIGN)
        x1_scales = held.tile([P, J], U8, name="x1_scales", align_bytes=ALIGN)
        halves = [slice(HALF * h, HALF * (h + 1)) for h in range(2)]
        weave(0, 2)
        weave(1, 2)
        for h in range(2):
            quantise(woven[h], x1_codes[:, halves[h]], x1_scales[:, halves[h]])
        looked = looked_tile("b_looked1", "cq3")
        for t in range(2, PACK):
            look_up_gated(looked, b_rows[t], t, idx5, sb_t, idx6, sh_t, bh_t)

        a_accs = []
        for t in range(PACK):
            acc = psum.tile([P, J], F32, name=f"a_acc{t}", tag=f"first{t}")
            if t == 0:
                for h in range(2):
                    first_product(acc[:, halves[h]], w_d, w_plane_d, x1_codes[:, halves[h]], x1_scales[:, halves[h]], t)
            else:
                first_product(acc[:], w_d, w_plane_d, x1_codes[:], x1_scales[:], t)
            a_accs.append(acc)

        gate(late_hid, looked, 2)
        a_rows = [rows_of(nc.scalar.copy, a_accs[0], "a_rows0")]
        a_rows.append(rows_of(nc.vector.tensor_copy, a_accs[1], "a_rows1"))
        late_q = quantise_hid(late_hid, "late")
        a_rows.extend(rows_of(nc.vector.tensor_copy, a_accs[t], f"a_rows{t}") for t in (2, 3))

        sums = {}
        for h in (1, 0):
            for n in range(2):
                acc = psum.tile([P, HALF], F32, name=f"p_acc{h}{n}", tag=f"p_acc{h}{n}")
                nc.tensor.matmul_mx(
                    out=acc[:],
                    lhsT=ws_w[:, 2 * P * n : 2 * P * (n + 1)].bitcast(FP4X4),
                    lhsT_scale=weight_planes[:, WS_AT + P * n : WS_AT + P * (n + 1)],
                    rhs=sx_w[:, 4 * HALF * h : 4 * HALF * (h + 1)].bitcast(FP8X4),
                    rhs_scale=weight_planes[:, SX_AT + HALF * h : SX_AT + HALF * (h + 1)],
                    start=True,
                    stop=False,
                )
                sums[h, n] = acc

        def second_stage(h, codes, scales):
            for n in range(2):
                nc.tensor.matmul_mx(
                    out=sums[h, n][:],
                    lhsT=wb_w[:, 2 * P * n : 2 * P * (n + 1)].bitcast(FP4X4),
                    lhsT_scale=weight_planes[:, WB_AT + P * n : WB_AT + P * (n + 1)],
                    rhs=codes[:].bitcast(FP8X4),
                    rhs_scale=scales[:],
                    start=False,
                    stop=True,
                )

        def out_of_psum(h, n, tag="", align=None):
            name = f"p_values{h}{n}"
            values = held.tile([P, HALF], F32, name=name, tag=tag or name, align_bytes=align)
            copy = nc.vector.tensor_copy if n == 0 else nc.scalar.copy
            copy(values[:], sums[h, n][:])
            return values

        def place(values, h, n):
            window = pages[n][:].indirect(idx7[:, 8 * h : 8 * (h + 1)])
            if n == 0:
                nc.vector.tensor_copy(window, values[:])
            else:
                nc.scalar.activation(out=window, in_=values[:], func=COPY)

        second_stage(1, *late_q)
        place(out_of_psum(1, 0, "late_values", ALIGN), 1, 0)
        hid = held.tile([P, HALF, PACK], BF16, name="hid", tag="late_values", align_bytes=ALIGN)
        for pair in range(2):
            looked = looked_tile(f"a_looked{pair}")
            for t in range(2 * pair, 2 * pair + 2):
                look_up_gated(looked, a_rows[t], t, idx3, sa_t, idx4, sg_t, bg_t)
            gate(hid, looked, 2 * pair)
        early_q = quantise_hid(hid, "early")
        place(out_of_psum(1, 1, "a_rows3"), 1, 1)
        second_stage(0, *early_q)
        for n in range(2):
            place(out_of_psum(0, n), 0, n)
            queue = nc.sync if n == 0 else nc.scalar
            queue.dma_start(out[P * n : P * (n + 1), :], pages[n][:])
